import numpy as np, ml_dtypes
CORES = [3,7,11,15,131,135,139,143]
N = 8
import mx_ref
BF = ml_dtypes.bfloat16
def entries(a):
    return np.ascontiguousarray(a.T).reshape(-1)
def table(e):
    return np.ascontiguousarray(np.reshape(e, (-1, 16)).T).astype(np.int32)
def f(rng, *shape):
    return mx_ref.flush((rng.standard_normal(shape, dtype=np.float32) * np.exp2(rng.integers(-2, 3, shape[:-1] + (1,)))).astype(BF))
def wide(rng, *shape, cols=0):
    v = rng.standard_normal(shape, dtype=np.float32) * np.exp2(rng.integers(-12, 13, shape)).astype(np.float32)
    if cols: v *= np.repeat(np.exp2(rng.integers(-cols, cols + 1, shape[:-2] + (1, shape[-1] // 4))) * (rng.random(shape[:-2] + (1, shape[-1] // 4)) > 0.0625), 4, axis=-1).astype(np.float32)
    return mx_ref.flush(v.astype(BF))
T = 512
def listed(a):
    k = np.full((2 * N, 128), -1)
    for s in range(2 * N):
        i = np.flatnonzero(a == s); k[s, :len(i)] = i
    return k.reshape(-1)
def lists(rng, one=False, absent=False, sort=False, alike=False):
    t, a, k = [], [], []; nobody = rng.integers(0, N)
    for r in range(N):
        if r == 0 or not alike:
            u = np.concatenate([rng.permutation(8)[:2] for q in range(N)])
            if absent:
                here = rng.permutation([q for q in range(N) if q != nobody])[:T // 256 + r % 3].tolist()
                u.reshape(N, 2)[[q for q in range(N) if q not in here]] = -1
            else: u[rng.permutation(2 * N)[:rng.integers(0, 5)]] = -1
        v = rng.permutation(np.flatnonzero(u >= 0))
        if one: e = np.concatenate([np.full(128, v[0]), np.resize(v[1:], T - 128)])
        else:
            room = np.zeros(2 * N, int); room[v] = rng.integers(0, 129, len(v))
            for s in v:
                if room.sum() < T: room[s] = 128
            e = np.repeat(np.arange(2 * N), room)
        e = rng.permutation(e)[:T]
        if sort: e = np.sort(e)
        t.append(table(u)); a.append(table(e)); k.append(table(listed(e)))
    return {"tab": np.stack(t), "ad": np.stack(a), "tok": np.stack(k)}
def setup_inputs(rng):
    return {"x": f(rng, N, 128, 4 * T), "wa": f(rng, N, 1024, 512), **lists(rng)}
def setup_inputs_absent(rng):
    return {**setup_inputs(rng), **lists(rng, absent=True)}
def setup_inputs_alike(rng):
    return {**setup_inputs(rng), **lists(rng, alike=True)}
def setup_inputs_one(rng):
    return {**setup_inputs(rng), **lists(rng, one=True)}
def setup_inputs_sorted(rng):
    return {**setup_inputs(rng), **lists(rng, sort=True)}
def setup_inputs_spread(rng):
    d = setup_inputs(rng); d["x"] = wide(rng, N, 128, 4 * T, cols=8); return d
def check_inputs(d):
    b = []
    for n in ("x", "wa"):
        v = np.abs(np.asarray(d[n]).astype(np.float32))
        if not ((v == 0) | ((v >= 2.0 ** -30) & (v <= 2.0 ** 30))).all(): b.append(n)
    for r in range(N):
        u, a, k = entries(d["tab"][r]), entries(d["ad"][r]), entries(d["tok"][r]); p = u.reshape(N, 2)
        if u.min() < -1 or u.max() > 7 or ((p[:, 0] == p[:, 1]) & (p[:, 0] >= 0)).any(): b.append("tab")
        if a.min() < 0 or a.max() >= 2 * N or (u[a] < 0).any() or np.bincount(a).max() > 128: b.append("ad")
        elif (k != listed(a)).any(): b.append("tok")
    return b
def reference(x, wa, tab, ad, tok):
    y = np.zeros((N, 128, T), np.float32)
    for r in range(N):
        u, a, X = entries(tab[r]), entries(ad[r]), mx_ref.quantize(x[r])
        for s in range(2 * N):
            i = np.flatnonzero(a == s)
            if len(i) == 0: continue
            A = wa[s // 2][128 * u[s]:128 * u[s] + 128]
            y[r][:, i] = mx_ref.matmul(mx_ref.quantize(A), X)[:, i]
    return {"y": y}

@@ -1,0 +1,362 @@
+from concourse.bass import DstId, RemoteDMATransfer, IndirectOffsetOnAxis
+from concourse.mybir import dt, AluOpType, ActivationFunctionType
+
+ORDER = (4, 2, 5, 3, 6, 7, 1)
+EARLY = 3
+SENDS = ((0,), (1, 2), (3, 4), (5,), (6,))
+S_TILES = {0: (1,), 1: (1,), 2: (0, 1), 3: (1,), 4: (1,), 5: (0, 1), 6: (1,)}
+X_EARLY = (2, 1)
+X_LATE = (3, 0)
+X_VEC = {2: (0, 1), 1: (0, 1), 3: (0,), 0: ()}
+PRODUCTS = (0, 1, 2, 3, 4, 7, 6, 5)
+
+SCRATCH = {
+    "tabd": ("dram", [128, 1], "int32"),
+    "landt": ("dram", [8, 128, 1], "int32"),
+    "orow": ("sbuf", [128, 16], "int32"),
+    "oall": ("sbuf", [128, 2], "int32"),
+    "om": ("sbuf", [128, 2], "int32"),
+    "oidx": ("sbuf", [128, 2], "int32"),
+    "own": ("sbuf", [128, 1024], "bfloat16"),
+    "mrow": ("sbuf", [128, 16], "int32"),
+    "mall": ("sbuf", [128, 16], "int32"),
+    "mf": ("sbuf", [128, 16], "float32"),
+    "ioa": ("sbuf", [128, 32], "int32"),
+    "iop": ("sbuf", [128, 32], "int32"),
+    "p15": ("sbuf", [128, 32], "int32"),
+    "obase": ("sbuf", [128, 32], "int32"),
+    "off": ("sbuf", [128, 32 * 14], "uint16"),
+    "win": ("sbuf", [128, 4096], "bfloat16"),
+    "ag": ("sbuf", [128, 1024 * 7], "bfloat16"),
+    "cs": ("sbuf", [128, 256 * 7], "float8_e4m3fn_x4"),
+    "ps": ("sbuf", [128, 256 * 7], "uint8"),
+    "cr": ("sbuf", [128, 256 * 7], "float8_e4m3fn_x4"),
+    "pr": ("sbuf", [128, 256 * 7], "uint8"),
+    "oc": ("sbuf", [128, 256], "float8_e4m3fn_x4"),
+    "op": ("sbuf", [128, 256], "uint8"),
+    "xin": ("sbuf", [128, 2048], "bfloat16"),
+    "tokt": ("sbuf", [128, 128], "int32"),
+    "offx": ("sbuf", [128, 128], "uint16"),
+    "xg": ("sbuf", [128, 8192], "bfloat16"),
+    "xq": ("sbuf", [128, 2048], "float8_e4m3fn_x4"),
+    "xp": ("sbuf", [128, 2048], "uint8"),
+    "adt": ("sbuf", [128, 32], "int32"),
+    "ab": ("sbuf", [128, 32], "bfloat16"),
+    "at": ("sbuf", [128, 32], "bfloat16"),
+    "adr": ("sbuf", [128, 512], "bfloat16"),
+    "adb": ("sbuf", [128, 512], "bfloat16"),
+    "sidi": ("sbuf", [128, 2], "int32"),
+    "sidf": ("sbuf", [128, 2], "float32"),
+    "eq": ("sbuf", [128, 512], "bfloat16"),
+    "cnt": ("sbuf", [128, 512], "bfloat16"),
+    "val": ("sbuf", [128, 512], "bfloat16"),
+    "trb": ("sbuf", [128, 512], "bfloat16"),
+    "msk": ("sbuf", [128, 512], "bfloat16"),
+    "sc": ("sbuf", [128, 512], "bfloat16"),
+    "r2": ("sbuf", [128, 32], "bfloat16"),
+    "ot": ("sbuf", [128, 32], "bfloat16"),
+    "adm": ("sbuf", [128, 32], "float32"),
+    "posf": ("sbuf", [128, 32], "float32"),
+    "posu": ("sbuf", [128, 32], "uint16"),
+    "acc": ("psum", [128, 4096], "float32"),
+    "res": ("sbuf", [128, 2048], "float32"),
+    "ysb": ("sbuf", [128, 512], "float32"),
+}
+SEMAPHORES = (["s_tabd", "s_orow", "s_tok", "s_x", "s_wa", "s_ad", "s_adr", "s_m1", "s_m2", "s_own", "s_y1", "s_y2",
+               "iota", "pbo", "pb1", "pb2", "pba", "vc", "offx", "oid", "atd", "qo", "pos", "fv", "fs", "tg1", "tg2", "sent"]
+              + ["of%d" % j for j in range(14)]
+              + ["%s%d" % (n, i) for n in ("sg", "vg", "q", "arr") for i in range(7)]
+              + ["%s%d" % (n, i) for n in ("xv", "xs", "xz") for i in range(4)]
+              + ["%s%d" % (n, i) for n in ("mv", "ms", "ev", "es") for i in range(8)])
+
+
+def bits(engines):
+    return sum(1 << e for e in engines)
+
+
+def rank_program(g, core, T, topo):
+    rank = T.rank_of(core)
+    if rank is None:
+        return
+    V, S, P, Y, sem = g.vector, g.scalar, g.tensor, g.sync, T.sem
+    add, mult, maxi = AluOpType.add, AluOpType.mult, AluOpType.max
+    copy = ActivationFunctionType.Copy
+    peers = [T.cores[rank ^ d] for d in ORDER]
+
+    def dst(i):
+        rid, pid = topo.addr(peers[i], core)
+        return DstId(rid=rid, pnc=pid)
+
+    off_chip = [e for i in range(7) if peers[i] not in topo.cores_of(core) for e in topo.engines(core, peers[i])]
+    wide = sorted(set(off_chip))
+    inner = {i: [e for e in topo.engines(core, peers[i]) if e not in wide] for i in range(7)}
+    vn = [0]
+
+    def chain(ins):
+        ins.then_inc(sem.vc, 1)
+        vn[0] += 1
+
+    def chained():
+        V.wait_ge(sem.vc, vn[0])
+
+    Y.dma_start(T.tabd[0:16, :], T.tab[:, :]).then_inc(sem.s_tabd, 16)
+    S.dma_start(T.tabd[16:128, :], T.tok[0:1, 0:112]).then_inc(sem.s_tabd, 16)
+    Y.dma_start(T.orow[0:1, 0:16], T.tab[:, :]).then_inc(sem.s_orow, 16)
+    for c in range(8):
+        Y.dma_start(T.tokt[16 * c:16 * c + 16, :], T.tok[:, :]).then_inc(sem.s_tok, 16)
+    S.dma_start(T.xin[:, :], T.x[:, :]).then_inc(sem.s_x, 16)
+    for m in range(8):
+        (Y if m < 4 else S).dma_start(T.win[:, 512 * m:512 * m + 512], T.wa[128 * m:128 * m + 128, :]).then_inc(sem.s_wa, 16)
+    for c in range(8):
+        Y.dma_start(T.adt[16 * c:16 * c + 16, :], T.ad[:, :]).then_inc(sem.s_ad, 16)
+    Y.wait_ge(sem.tg1, EARLY)
+    Y.dma_start(T.mrow[0:1, 0:2 * EARLY], T.landt[0:EARLY, 2 * rank:2 * rank + 2, :]).then_inc(sem.s_m1, 16)
+    Y.wait_ge(sem.tg2, (7 - EARLY) * len(wide))
+    Y.dma_start(T.mrow[0:1, 2 * EARLY:14], T.landt[EARLY:7, 2 * rank:2 * rank + 2, :]).then_inc(sem.s_m2, 16)
+    Y.wait_ge(sem.atd, 1)
+    Y.dma_start(T.adr[0:1, 0:512], T.at[0:32, 0:16]).then_inc(sem.s_adr, 16)
+
+    g.iota(T.ioa[:, 0:32], [[16, 32]], 0, 0).then_inc(sem.iota, 1)
+    g.iota(T.iop[:, 0:32], [[0, 32]], 0, 1).then_inc(sem.iota, 1)
+    g.wait_ge(sem.s_tabd, 32)
+    nsent = 0
+    for lo, hi, engs, name in ((0, EARLY, wide[:1], "tg1"), (EARLY, 7, wide, "tg2")):
+        g.remote_dma_fused([RemoteDMATransfer(dst_ids=[dst(i) for i in range(lo, hi)], dma_engine_mask=bits(engs),
+                                              remote_sem=sem[name], srcs=[T.tabd[:, :]],
+                                              dsts=[T.landt[i] for i in range(lo, hi)])], local_sem=sem.sent)
+        nsent += len(engs)
+    g.wait_ge(sem.s_orow, 16)
+    g.partition_broadcast(T.oall[:, 0:2], T.orow[0:1, 2 * rank:2 * rank + 2], 128).then_inc(sem.pbo, 1)
+    g.wait_ge(sem.oid, 1)
+    for k in range(2):
+        g.indirect_dma_start(T.own[:, 512 * k:512 * k + 512], None, T.wa[:],
+                             IndirectOffsetOnAxis(ap=T.oidx[:, k:k + 1], axis=0), bounds_check=1023).then_inc(sem.s_own, 16)
+    g.wait_ge(sem.s_m1, 16)
+    g.partition_broadcast(T.mall[:, 0:2 * EARLY], T.mrow[0:1, 0:2 * EARLY], 128).then_inc(sem.pb1, 1)
+    g.wait_ge(sem.s_m2, 16)
+    g.partition_broadcast(T.mall[:, 2 * EARLY:14], T.mrow[0:1, 2 * EARLY:14], 128).then_inc(sem.pb2, 1)
+    arrived = {}
+    for group in SENDS:
+        for i in group:
+            g.wait_ge(sem["q%d" % i], 1)
+        per = len(wide) // len(group)
+        mine = {}
+        for n, i in enumerate(group):
+            mine[i] = wide[per * n:per * n + per] if not inner[i] else inner[i][:len(inner[i]) // 2]
+            arrived[i] = 2 * len(mine[i])
+        for part in ("codes", "plane"):
+            moves = []
+            for i in group:
+                a, b = 256 * i, 256 * i + 256
+                if part == "codes":
+                    src, to = T.cs[:, a:b].bitcast(dt.uint8), T.cr[:, a:b].bitcast(dt.uint8)
+                else:
+                    src, to = T.ps[:, a:b], T.pr[:, a:b]
+                moves.append(RemoteDMATransfer(dst_ids=[dst(i)], dma_engine_mask=bits(mine[i]),
+                                               remote_sem=sem["arr%d" % i], srcs=[src], dsts=[to]))
+                nsent += len(mine[i])
+            g.remote_dma_fused(moves, local_sem=sem.sent)
+    g.wait_ge(sem.s_adr, 16)
+    g.partition_broadcast(T.adb[:, 0:512], T.adr[0:1, 0:512], 128).then_inc(sem.pba, 1)
+    g.wait_ge(sem.sent, nsent)
+
+    def gather_x(eng, h, t):
+        b = (rank & ~1) ^ (2 * h)
+        out, win = T.xg[:, 2048 * h + t:2048 * h + 2048:4], T.xin[:, t:2048].indirect(T.offx[:, 16 * b:16 * b + 32])
+        if eng == "v":
+            V.tensor_copy(out, win).then_inc(sem["xv%d" % h], 1)
+        else:
+            S.activation(out, win, copy).then_inc(sem["xs%d" % h], 1)
+
+    def quant_x(h):
+        if X_VEC[h]:
+            V.wait_ge(sem["xv%d" % h], len(X_VEC[h]))
+        if len(X_VEC[h]) < 4:
+            V.wait_ge(sem["xs%d" % h], 4 - len(X_VEC[h]))
+        V.quantize_mx(T.xq[:, 512 * h:512 * h + 512], T.xp[:, 512 * h:512 * h + 512],
+                      T.xg[:, 2048 * h:2048 * h + 2048]).then_inc(sem["xz%d" % h], 1)
+
+    def tile_window(j):
+        return T.win[:, 0:4096].indirect(T.off[:, 32 * j:32 * j + 32])
+
+    def evacuate(eng, n):
+        i, k = PRODUCTS[n], 0 if eng == "v" else 1
+        src = rank if i == 7 else rank ^ ORDER[i]
+        bank = 2 * (n % 4) + k
+        out, acc = T.res[:, 128 * (2 * src + k):128 * (2 * src + k) + 128], T.acc[:, 512 * bank:512 * bank + 128]
+        if eng == "v":
+            V.wait_ge(sem["mv%d" % n], 1)
+            V.tensor_copy(out, acc).then_inc(sem["ev%d" % n], 1)
+        else:
+            S.wait_ge(sem["ms%d" % n], 1)
+            S.activation(out, acc, copy).then_inc(sem["es%d" % n], 1)
+
+    chain(V.memset(T.msk[:, 0:512], 1.0))
+    chained()
+    chain(V.memset(T.msk[:, 0:512:32], 0.0))
+    V.wait_ge(sem.iota, 2)
+    chain(V.tensor_scalar(T.p15[:, 0:32], T.iop[:, 0:32], 15, None, AluOpType.bitwise_and))
+    chain(V.tensor_scalar(T.sidi[:, 0:1], T.iop[:, 0:1], 31, None, AluOpType.bitwise_and))
+    chained()
+    chain(V.tensor_tensor(T.obase[:, 0:32], T.ioa[:, 0:32], T.p15[:, 0:32], add))
+    chain(V.tensor_copy(T.sidf[:, 0:1], T.sidi[:, 0:1]))
+    V.wait_ge(sem.s_tok, 128)
+    V.tensor_scalar(T.offx[:, 0:128], T.tokt[:, 0:128], 0, 4, maxi, mult).then_inc(sem.offx, 1)
+    V.wait_ge(sem.offx, 1)
+    V.wait_ge(sem.s_x, 16)
+    first = True
+    for h in X_EARLY:
+        for t in X_VEC[h]:
+            gather_x("v", h, t)
+            if first:
+                first = False
+                V.wait_ge(sem.pbo, 1)
+                chain(V.tensor_scalar(T.om[:, 0:2], T.oall[:, 0:2], 0, 128, maxi, mult))
+                chained()
+                V.tensor_tensor(T.oidx[:, 0:2], T.om[:, 0:2], T.iop[:, 0:2], add).then_inc(sem.oid, 1)
+    V.wait_ge(sem.s_ad, 128)
+    chain(V.tensor_copy(T.ab[:, 0:32], T.adt[:, 0:32]))
+    chain(V.tensor_scalar(T.adm[:, 0:32], T.adt[:, 0:32], 128, -1, mult, add))
+    chained()
+    V.transpose(T.at[:, 0:32], T.ab[:, 0:32]).then_inc(sem.atd, 1)
+
+    def load_table(n, a, b):
+        V.wait_ge(sem["pb%d" % n], 1)
+        chain(V.tensor_scalar(T.mf[:, a:b], T.mall[:, a:b], 0, 512, maxi, mult))
+        chained()
+
+    def offsets_of(i, who):
+        for k in range(2):
+            j = 2 * i + k
+            if (k in S_TILES[i]) == (who == "s"):
+                V.tensor_scalar(T.off[:, 32 * j:32 * j + 32], T.obase[:, 0:32], T.mf[:, j:j + 1], None, add).then_inc(sem["of%d" % j], 1)
+
+    def gather_v(i):
+        for k in range(2):
+            if k not in S_TILES[i]:
+                j = 2 * i + k
+                V.wait_ge(sem["of%d" % j], 1)
+                V.tensor_copy(T.ag[:, 512 * j:512 * j + 512], tile_window(j)).then_inc(sem["vg%d" % i], 1)
+
+    def quant_tile(i):
+        if len(S_TILES[i]) < 2:
+            V.wait_ge(sem["vg%d" % i], 2 - len(S_TILES[i]))
+        V.wait_ge(sem["sg%d" % i], len(S_TILES[i]))
+        V.quantize_mx(T.cs[:, 256 * i:256 * i + 256], T.ps[:, 256 * i:256 * i + 256],
+                      T.ag[:, 1024 * i:1024 * i + 1024]).then_inc(sem["q%d" % i], 1)
+
+    load_table(1, 0, 2 * EARLY)
+    offsets_of(0, "s")
+    offsets_of(0, "v")
+    offsets_of(1, "s")
+    V.wait_ge(sem.s_wa, 128)
+    gather_v(0)
+    offsets_of(1, "v")
+    offsets_of(2, "s")
+    quant_tile(0)
+    gather_v(1)
+    load_table(2, 2 * EARLY, 14)
+    offsets_of(3, "s")
+    offsets_of(3, "v")
+    quant_tile(1)
+    gather_v(3)
+    offsets_of(4, "s")
+    offsets_of(4, "v")
+    offsets_of(5, "s")
+    quant_tile(2)
+    gather_v(4)
+    offsets_of(6, "s")
+    offsets_of(6, "v")
+    quant_tile(3)
+    quant_tile(4)
+    gather_v(6)
+    quant_tile(5)
+    quant_tile(6)
+
+    for h in X_EARLY:
+        quant_x(h)
+    V.wait_ge(sem.s_own, 32)
+    V.quantize_mx(T.oc[:, 0:256], T.op[:, 0:256], T.own[:, 0:1024]).then_inc(sem.qo, 1)
+    for h in X_LATE:
+        for t in X_VEC[h]:
+            gather_x("v", h, t)
+    evacuate("v", 0)
+    evacuate("v", 1)
+    V.wait_ge(sem.pba, 1)
+    chain(V.tensor_scalar(T.eq[:, 0:512], T.adb[:, 0:512], T.sidf[:, 0:1], None, AluOpType.is_equal))
+    chained()
+    chain(V.tensor_tensor_scan(T.cnt[:, 0:512], T.eq[:, 0:512], T.eq[:, 0:512], 0.0, add, maxi))
+    chained()
+    for b in range(16):
+        chain(V.tensor_tensor(T.val[:, 32 * b:32 * b + 32], T.eq[:, b:512:16], T.cnt[:, b:512:16], mult))
+    chained()
+    chain(V.transpose(T.trb[:, 0:512], T.val[:, 0:512]))
+    chained()
+    chain(V.tensor_tensor_scan(T.sc[:, 0:512], T.msk[:, 0:512], T.trb[:, 0:512], 0.0, mult, add))
+    chained()
+    for c in range(2):
+        chain(V.tensor_copy(T.r2[:, 16 * c:16 * c + 16], T.sc[:, 31:512:32]))
+    chained()
+    chain(V.transpose(T.ot[:, 0:32], T.r2[:, 0:32]))
+    chained()
+    chain(V.tensor_tensor(T.posf[:, 0:32], T.adm[:, 0:32], T.ot[:, 0:32], add))
+    chained()
+    V.tensor_copy(T.posu[:, 0:32], T.posf[:, 0:32]).then_inc(sem.pos, 1)
+    for h in X_LATE:
+        quant_x(h)
+    for n in range(2, 8):
+        evacuate("v", n)
+
+    S.wait_ge(sem.offx, 1)
+    S.wait_ge(sem.s_x, 16)
+    for h in X_EARLY:
+        for t in range(4):
+            if t not in X_VEC[h]:
+                gather_x("s", h, t)
+    S.wait_ge(sem.s_wa, 128)
+    for i in range(7):
+        for k in S_TILES[i]:
+            j = 2 * i + k
+            S.wait_ge(sem["of%d" % j], 1)
+            S.activation(T.ag[:, 512 * j:512 * j + 512], tile_window(j), copy).then_inc(sem["sg%d" % i], 1)
+    for h in X_LATE:
+        for t in range(4):
+            if t not in X_VEC[h]:
+                gather_x("s", h, t)
+    for n in range(8):
+        evacuate("s", n)
+
+    seen = set()
+    for n, i in enumerate(PRODUCTS):
+        d = 0 if i == 7 else ORDER[i]
+        if d >> 1 not in seen:
+            seen.add(d >> 1)
+            P.wait_ge(sem["xz%d" % (d >> 1)], 1)
+        if i == 7:
+            P.wait_ge(sem.qo, 1)
+        else:
+            P.wait_ge(sem["arr%d" % i], arrived[i])
+        for k in range(2):
+            bank = 2 * (n % 4) + k
+            if n >= 4:
+                P.wait_ge(sem["%s%d" % (("ev", "es")[k], n - 4)], 1)
+            a = 512 * (d >> 1) + 256 * ((rank ^ d) & 1) + 128 * k
+            c = 128 * k if i == 7 else 256 * i + 128 * k
+            w, ws = (T.oc, T.op) if i == 7 else (T.cr, T.pr)
+            P.matmul_mx(T.acc[:, 512 * bank:512 * bank + 128], w[:, c:c + 128], ws[:, c:c + 128],
+                        T.xq[:, a:a + 128], T.xp[:, a:a + 128], True, True).then_inc(sem["%s%d" % (("mv", "ms")[k], n)], 1)
+
+    for eng in (V, S):
+        eng.wait_ge(sem.pos, 1)
+        for n in range(8):
+            eng.wait_ge(sem["ev%d" % n], 1)
+            eng.wait_ge(sem["es%d" % n], 1)
+    V.tensor_copy(T.ysb[:, 0:256], T.res[:, 0:2048].indirect(T.posu[:, 0:16])).then_inc(sem.fv, 1)
+    S.activation(T.ysb[:, 256:512], T.res[:, 0:2048].indirect(T.posu[:, 16:32]), copy).then_inc(sem.fs, 1)
+    Y.wait_ge(sem.fv, 1)
+    Y.dma_start(T.y[:, 0:256], T.ysb[:, 0:256]).then_inc(sem.s_y1, 16)
+    S.wait_ge(sem.fs, 1)
+    S.dma_start(T.y[:, 256:512], T.ysb[:, 256:512]).then_inc(sem.s_y2, 16)
+    Y.wait_ge(sem.s_y1, 16)
+    S.wait_ge(sem.s_y2, 16)
+    V.wait_ge(sem.vc, vn[0])

@@ -2,51 +2,52 @@ from concourse.bass import DstId, RemoteDMATransfer, IndirectOffsetOnAxis
 from concourse.mybir import dt, AluOpType, ActivationFunctionType
 
 ORDER = (4, 2, 5, 3, 6, 7, 1)
-EARLY = 3
+RELAY = ()
+TABLES = ((0, 1), (2, 3), (4, 5, 6))
 SENDS = ((0,), (1, 2), (3, 4), (5,), (6,))
-S_TILES = {0: (1,), 1: (1,), 2: (0, 1), 3: (1,), 4: (1,), 5: (0, 1), 6: (1,)}
-X_EARLY = (2, 1)
-X_LATE = (3, 0)
-X_VEC = {2: (0, 1), 1: (0, 1), 3: (0,), 0: ()}
-PRODUCTS = (0, 1, 2, 3, 4, 7, 6, 5)
+PRODUCTS = (0, 1, 2, 3, 4, 6, 7, 5)
+VECTOR = ("x.2.0 x.2.1 x.1.0 x.1.1 o.0 o.1 v.0.0 o.2 q.0 v.1.0 o.3 q.1 v.3.0 o.4 q.2 o.5 v.4.0 q.3 o.6 q.4 v.6.0 q.5 q.6 "
+          "z.2 z.1 w x.3.0 e.0.0 r z.3 z.0 e.1.0 e.2.0 e.3.0 e.4.0 e.5.0 e.6.0 e.7.0")
+SCALAR = ("x.2.2 x.2.3 x.1.2 x.1.3 v.0.1 v.1.1 v.2.0 v.2.1 v.3.1 v.4.1 v.5.0 v.5.1 v.6.1 x.3.1 x.3.2 x.3.3 x.0.0 x.0.1 x.0.2 x.0.3 "
+          "e.0.1 e.1.1 e.2.1 e.3.1 e.4.1 e.5.1 e.6.1 e.7.1")
+GPSIMD = "i.0 i.1 s.0 s.1 s.2 s.3 s.4"
+LOADS_SYNC = "o a.0 t.0 t.2 t.4 t.6 w.0 w.2 w.4 w.6"
+LOADS_SCALAR = "a.1 t.1 t.3 t.5 t.7 x w.1 w.3 w.5 w.7"
 
 SCRATCH = {
-    "tabd": ("dram", [128, 1], "int32"),
-    "landt": ("dram", [8, 128, 1], "int32"),
     "orow": ("sbuf", [128, 16], "int32"),
-    "oall": ("sbuf", [128, 2], "int32"),
+    "tall": ("sbuf", [128, 16], "int32"),
+    "tbl": ("sbuf", [128, 16], "bfloat16"),
+    "mrec": ("sbuf", [128, 16], "bfloat16"),
     "om": ("sbuf", [128, 2], "int32"),
     "oidx": ("sbuf", [128, 2], "int32"),
     "own": ("sbuf", [128, 1024], "bfloat16"),
-    "mrow": ("sbuf", [128, 16], "int32"),
-    "mall": ("sbuf", [128, 16], "int32"),
-    "mf": ("sbuf", [128, 16], "float32"),
     "ioa": ("sbuf", [128, 32], "int32"),
     "iop": ("sbuf", [128, 32], "int32"),
+    "part": ("sbuf", [128, 2], "float32"),
     "p15": ("sbuf", [128, 32], "int32"),
     "obase": ("sbuf", [128, 32], "int32"),
     "off": ("sbuf", [128, 32 * 14], "uint16"),
     "win": ("sbuf", [128, 4096], "bfloat16"),
-    "ag": ("sbuf", [128, 1024 * 7], "bfloat16"),
+    "agt": ("sbuf", [128, 1024 * 7], "bfloat16"),
     "cs": ("sbuf", [128, 256 * 7], "float8_e4m3fn_x4"),
     "ps": ("sbuf", [128, 256 * 7], "uint8"),
     "cr": ("sbuf", [128, 256 * 7], "float8_e4m3fn_x4"),
     "pr": ("sbuf", [128, 256 * 7], "uint8"),
+    "hc": ("sbuf", [128, 256], "float8_e4m3fn_x4"),
+    "hp": ("sbuf", [128, 256], "uint8"),
     "oc": ("sbuf", [128, 256], "float8_e4m3fn_x4"),
     "op": ("sbuf", [128, 256], "uint8"),
     "xin": ("sbuf", [128, 2048], "bfloat16"),
     "tokt": ("sbuf", [128, 128], "int32"),
     "offx": ("sbuf", [128, 128], "uint16"),
-    "xg": ("sbuf", [128, 8192], "bfloat16"),
+    "xgt": ("sbuf", [128, 8192], "bfloat16"),
     "xq": ("sbuf", [128, 2048], "float8_e4m3fn_x4"),
     "xp": ("sbuf", [128, 2048], "uint8"),
     "adt": ("sbuf", [128, 32], "int32"),
     "ab": ("sbuf", [128, 32], "bfloat16"),
     "at": ("sbuf", [128, 32], "bfloat16"),
-    "adr": ("sbuf", [128, 512], "bfloat16"),
     "adb": ("sbuf", [128, 512], "bfloat16"),
-    "sidi": ("sbuf", [128, 2], "int32"),
-    "sidf": ("sbuf", [128, 2], "float32"),
     "eq": ("sbuf", [128, 512], "bfloat16"),
     "cnt": ("sbuf", [128, 512], "bfloat16"),
     "val": ("sbuf", [128, 512], "bfloat16"),
@@ -57,39 +58,78 @@ SCRATCH = {
     "ot": ("sbuf", [128, 32], "bfloat16"),
     "adm": ("sbuf", [128, 32], "float32"),
     "posf": ("sbuf", [128, 32], "float32"),
+    "posl": ("sbuf", [128, 32], "uint16"),
     "posu": ("sbuf", [128, 32], "uint16"),
     "acc": ("psum", [128, 4096], "float32"),
     "res": ("sbuf", [128, 2048], "float32"),
     "ysb": ("sbuf", [128, 512], "float32"),
 }
-SEMAPHORES = (["s_tabd", "s_orow", "s_tok", "s_x", "s_wa", "s_ad", "s_adr", "s_m1", "s_m2", "s_own", "s_y1", "s_y2",
-               "iota", "pbo", "pb1", "pb2", "pba", "vc", "offx", "oid", "atd", "qo", "pos", "fv", "fs", "tg1", "tg2", "sent"]
-              + ["of%d" % j for j in range(14)]
-              + ["%s%d" % (n, i) for n in ("sg", "vg", "q", "arr") for i in range(7)]
-              + ["%s%d" % (n, i) for n in ("xv", "xs", "xz") for i in range(4)]
-              + ["%s%d" % (n, i) for n in ("mv", "ms", "ev", "es") for i in range(8)])
+SEMAPHORES = (["s_orow", "s_tok", "s_x", "s_wa", "s_ad", "s_adb", "s_own", "s_pos", "s_y1", "s_y2", "hrc", "hrp",
+               "iota", "pbo", "vc", "tbr", "offx", "oid", "atd", "qo", "pos", "fv", "fs", "sent"]
+              + ["%s%d" % (n, i) for n in ("tb", "of", "tg", "q", "arr") for i in range(7)]
+              + ["%s%d" % (n, i) for n in ("xg", "xz") for i in range(4)]
+              + ["%s%d" % (n, i) for n in ("m0_", "m1_", "e0_", "e1_") for i in range(8)])
 
 
 def bits(engines):
     return sum(1 << e for e in engines)
 
 
+def address(topo, to, core):
+    rid, pid = topo.addr(to, core)
+    return DstId(rid=rid, pnc=pid)
+
+
+def engine_sets(T, topo, core):
+    near = topo.cores_of(core)
+    wide = sorted({e for c in T.cores if c not in near for e in topo.engines(core, c)})
+    inner = sorted({e for c in near if c != core for e in topo.engines(core, c)} - set(wide))
+    return wide, inner[:len(inner) // 2]
+
+
+def helpers(T, topo, rank):
+    core, taken = T.cores[rank], {}
+    for i in RELAY:
+        to = T.cores[rank ^ ORDER[i]]
+        free = [h for h in topo.cores_of(core) if h not in T.cores and h not in taken.values()
+                and topo.die(h) == topo.die(core) and topo.may_write(core, h) and topo.may_write(h, to)]
+        taken[i] = min(free, key=lambda h: (sum(topo.may_write(h, c) for c in T.cores), h))
+    return taken
+
+
+def relay_program(g, core, T, topo):
+    for rank in range(len(T.cores)):
+        for i, h in helpers(T, topo, rank).items():
+            if h == core:
+                to = T.cores[rank ^ ORDER[i]]
+                out, here = topo.engines(core, to), len(engine_sets(T, topo, T.cores[rank])[1])
+                for name, a, b in (("hrc", T.hc[:, 0:256].bitcast(dt.uint8), T.cr[:, 256 * i:256 * i + 256].bitcast(dt.uint8)),
+                                   ("hrp", T.hp[:, 0:256], T.pr[:, 256 * i:256 * i + 256])):
+                    g.wait_ge(T.sem[name], here)
+                    g.remote_dma_fused([RemoteDMATransfer(dst_ids=[address(topo, to, core)], dma_engine_mask=bits(out),
+                                                          remote_sem=T.sem["arr%d" % i], srcs=[a], dsts=[b])], local_sem=T.sem.sent)
+                g.wait_ge(T.sem.sent, 2 * len(out))
+
+
 def rank_program(g, core, T, topo):
     rank = T.rank_of(core)
     if rank is None:
+        relay_program(g, core, T, topo)
         return
     V, S, P, Y, sem = g.vector, g.scalar, g.tensor, g.sync, T.sem
     add, mult, maxi = AluOpType.add, AluOpType.mult, AluOpType.max
     copy = ActivationFunctionType.Copy
     peers = [T.cores[rank ^ d] for d in ORDER]
+    helper = helpers(T, topo, rank)
+    wide, inner = engine_sets(T, topo, core)
 
-    def dst(i):
-        rid, pid = topo.addr(peers[i], core)
-        return DstId(rid=rid, pnc=pid)
+    def share(group, relays=()):
+        out = [i for i in group if peers[i] not in topo.cores_of(core) and i not in relays]
+        per = len(wide) // max(1, len(out))
+        m = {i: wide[per * n:per * n + per] for n, i in enumerate(out)}
+        m.update({i: inner for i in group if i not in out})
+        return m
 
-    off_chip = [e for i in range(7) if peers[i] not in topo.cores_of(core) for e in topo.engines(core, peers[i])]
-    wide = sorted(set(off_chip))
-    inner = {i: [e for e in topo.engines(core, peers[i]) if e not in wide] for i in range(7)}
     vn = [0]
 
     def chain(ins):
@@ -99,239 +139,178 @@ def rank_program(g, core, T, topo):
     def chained():
         V.wait_ge(sem.vc, vn[0])
 
-    Y.dma_start(T.tabd[0:16, :], T.tab[:, :]).then_inc(sem.s_tabd, 16)
-    S.dma_start(T.tabd[16:128, :], T.tok[0:1, 0:112]).then_inc(sem.s_tabd, 16)
-    Y.dma_start(T.orow[0:1, 0:16], T.tab[:, :]).then_inc(sem.s_orow, 16)
-    for c in range(8):
-        Y.dma_start(T.tokt[16 * c:16 * c + 16, :], T.tok[:, :]).then_inc(sem.s_tok, 16)
-    S.dma_start(T.xin[:, :], T.x[:, :]).then_inc(sem.s_x, 16)
-    for m in range(8):
-        (Y if m < 4 else S).dma_start(T.win[:, 512 * m:512 * m + 512], T.wa[128 * m:128 * m + 128, :]).then_inc(sem.s_wa, 16)
-    for c in range(8):
-        Y.dma_start(T.adt[16 * c:16 * c + 16, :], T.ad[:, :]).then_inc(sem.s_ad, 16)
-    Y.wait_ge(sem.tg1, EARLY)
-    Y.dma_start(T.mrow[0:1, 0:2 * EARLY], T.landt[0:EARLY, 2 * rank:2 * rank + 2, :]).then_inc(sem.s_m1, 16)
-    Y.wait_ge(sem.tg2, (7 - EARLY) * len(wide))
-    Y.dma_start(T.mrow[0:1, 2 * EARLY:14], T.landt[EARLY:7, 2 * rank:2 * rank + 2, :]).then_inc(sem.s_m2, 16)
+    for eng, words in ((Y, LOADS_SYNC), (S, LOADS_SCALAR)):
+        for word in words.split():
+            w = word.split(".")
+            c = int(w[1]) if len(w) > 1 else 0
+            if w[0] == "o":
+                eng.dma_start(T.orow[0:1, 0:16], T.tab[:, :]).then_inc(sem.s_orow, 16)
+            elif w[0] == "t":
+                eng.dma_start(T.tokt[16 * c:16 * c + 16, :], T.tok[:, :]).then_inc(sem.s_tok, 16)
+            elif w[0] == "a":
+                eng.dma_start(T.adt[16 * c:16 * c + 16, :], T.ad[:, :]).then_inc(sem.s_ad, 16)
+            elif w[0] == "x":
+                eng.dma_start(T.xin[:, :], T.x[:, :]).then_inc(sem.s_x, 16)
+            else:
+                eng.dma_start(T.win[:, 512 * c:512 * c + 512], T.wa[128 * c:128 * c + 128, :]).then_inc(sem.s_wa, 16)
     Y.wait_ge(sem.atd, 1)
-    Y.dma_start(T.adr[0:1, 0:512], T.at[0:32, 0:16]).then_inc(sem.s_adr, 16)
+    for s in range(16):
+        Y.dma_start(T.adb[s:s + 1, 0:512], T.at[0:32, 0:16]).then_inc(sem.s_adb, 16)
+    Y.wait_ge(sem.pos, 1)
+    for c in range(4):
+        Y.dma_start(T.posu[32 * c:32 * c + 32, :], T.posl[0:32, :]).then_inc(sem.s_pos, 16)
 
     g.iota(T.ioa[:, 0:32], [[16, 32]], 0, 0).then_inc(sem.iota, 1)
     g.iota(T.iop[:, 0:32], [[0, 32]], 0, 1).then_inc(sem.iota, 1)
-    g.wait_ge(sem.s_tabd, 32)
-    nsent = 0
-    for lo, hi, engs, name in ((0, EARLY, wide[:1], "tg1"), (EARLY, 7, wide, "tg2")):
-        g.remote_dma_fused([RemoteDMATransfer(dst_ids=[dst(i) for i in range(lo, hi)], dma_engine_mask=bits(engs),
-                                              remote_sem=sem[name], srcs=[T.tabd[:, :]],
-                                              dsts=[T.landt[i] for i in range(lo, hi)])], local_sem=sem.sent)
-        nsent += len(engs)
     g.wait_ge(sem.s_orow, 16)
-    g.partition_broadcast(T.oall[:, 0:2], T.orow[0:1, 2 * rank:2 * rank + 2], 128).then_inc(sem.pbo, 1)
-    g.wait_ge(sem.oid, 1)
-    for k in range(2):
-        g.indirect_dma_start(T.own[:, 512 * k:512 * k + 512], None, T.wa[:],
-                             IndirectOffsetOnAxis(ap=T.oidx[:, k:k + 1], axis=0), bounds_check=1023).then_inc(sem.s_own, 16)
-    g.wait_ge(sem.s_m1, 16)
-    g.partition_broadcast(T.mall[:, 0:2 * EARLY], T.mrow[0:1, 0:2 * EARLY], 128).then_inc(sem.pb1, 1)
-    g.wait_ge(sem.s_m2, 16)
-    g.partition_broadcast(T.mall[:, 2 * EARLY:14], T.mrow[0:1, 2 * EARLY:14], 128).then_inc(sem.pb2, 1)
-    arrived = {}
-    for group in SENDS:
+    g.partition_broadcast(T.tall[:, 0:16], T.orow[0:1, 0:16], 128).then_inc(sem.pbo, 1)
+    g.wait_ge(sem.tbr, 1)
+    nsent = 0
+    tables, arrived = {}, {}
+    for group in TABLES:
+        moves = []
+        for i, engs in share(group).items():
+            p = rank ^ ORDER[i]
+            moves.append(RemoteDMATransfer(dst_ids=[address(topo, peers[i], core)], dma_engine_mask=bits(engs),
+                                           remote_sem=sem["tb%d" % i], srcs=[T.tbl[:, 2 * p:2 * p + 2]],
+                                           dsts=[T.mrec[:, 2 * i:2 * i + 2]]))
+            tables[i] = len(engs)
+            nsent += len(engs)
+        g.remote_dma_fused(moves, local_sem=sem.sent)
+    for word in GPSIMD.split():
+        w = word.split(".")
+        if w[0] == "i":
+            k = int(w[1])
+            g.wait_ge(sem.oid, 1)
+            g.indirect_dma_start(T.own[:, 512 * k:512 * k + 512], None, T.wa[:],
+                                 IndirectOffsetOnAxis(ap=T.oidx[:, k:k + 1], axis=0), bounds_check=1023).then_inc(sem.s_own, 16)
+            continue
+        group = SENDS[int(w[1])]
         for i in group:
             g.wait_ge(sem["q%d" % i], 1)
-        per = len(wide) // len(group)
-        mine = {}
-        for n, i in enumerate(group):
-            mine[i] = wide[per * n:per * n + per] if not inner[i] else inner[i][:len(inner[i]) // 2]
-            arrived[i] = 2 * len(mine[i])
-        for part in ("codes", "plane"):
+        for codes in (True, False):
             moves = []
-            for i in group:
-                a, b = 256 * i, 256 * i + 256
-                if part == "codes":
-                    src, to = T.cs[:, a:b].bitcast(dt.uint8), T.cr[:, a:b].bitcast(dt.uint8)
+            for i, engs in share(group, RELAY).items():
+                a = (T.cs if codes else T.ps)[:, 256 * i:256 * i + 256]
+                if i in RELAY:
+                    b, to, name = (T.hc if codes else T.hp)[:, 0:256], helper[i], "hrc" if codes else "hrp"
+                    arrived[i] = 2 * len(topo.engines(helper[i], peers[i]))
                 else:
-                    src, to = T.ps[:, a:b], T.pr[:, a:b]
-                moves.append(RemoteDMATransfer(dst_ids=[dst(i)], dma_engine_mask=bits(mine[i]),
-                                               remote_sem=sem["arr%d" % i], srcs=[src], dsts=[to]))
-                nsent += len(mine[i])
+                    b, to, name = (T.cr if codes else T.pr)[:, 256 * i:256 * i + 256], peers[i], "arr%d" % i
+                    arrived[i] = 2 * len(engs)
+                if codes:
+                    a, b = a.bitcast(dt.uint8), b.bitcast(dt.uint8)
+                moves.append(RemoteDMATransfer(dst_ids=[address(topo, to, core)], dma_engine_mask=bits(engs),
+                                               remote_sem=sem[name], srcs=[a], dsts=[b]))
+                nsent += len(engs)
             g.remote_dma_fused(moves, local_sem=sem.sent)
-    g.wait_ge(sem.s_adr, 16)
-    g.partition_broadcast(T.adb[:, 0:512], T.adr[0:1, 0:512], 128).then_inc(sem.pba, 1)
     g.wait_ge(sem.sent, nsent)
 
-    def gather_x(eng, h, t):
-        b = (rank & ~1) ^ (2 * h)
-        out, win = T.xg[:, 2048 * h + t:2048 * h + 2048:4], T.xin[:, t:2048].indirect(T.offx[:, 16 * b:16 * b + 32])
-        if eng == "v":
-            V.tensor_copy(out, win).then_inc(sem["xv%d" % h], 1)
-        else:
-            S.activation(out, win, copy).then_inc(sem["xs%d" % h], 1)
-
-    def quant_x(h):
-        if X_VEC[h]:
-            V.wait_ge(sem["xv%d" % h], len(X_VEC[h]))
-        if len(X_VEC[h]) < 4:
-            V.wait_ge(sem["xs%d" % h], 4 - len(X_VEC[h]))
-        V.quantize_mx(T.xq[:, 512 * h:512 * h + 512], T.xp[:, 512 * h:512 * h + 512],
-                      T.xg[:, 2048 * h:2048 * h + 2048]).then_inc(sem["xz%d" % h], 1)
-
-    def tile_window(j):
-        return T.win[:, 0:4096].indirect(T.off[:, 32 * j:32 * j + 32])
-
-    def evacuate(eng, n):
-        i, k = PRODUCTS[n], 0 if eng == "v" else 1
-        src = rank if i == 7 else rank ^ ORDER[i]
-        bank = 2 * (n % 4) + k
-        out, acc = T.res[:, 128 * (2 * src + k):128 * (2 * src + k) + 128], T.acc[:, 512 * bank:512 * bank + 128]
-        if eng == "v":
-            V.wait_ge(sem["mv%d" % n], 1)
-            V.tensor_copy(out, acc).then_inc(sem["ev%d" % n], 1)
-        else:
-            S.wait_ge(sem["ms%d" % n], 1)
-            S.activation(out, acc, copy).then_inc(sem["es%d" % n], 1)
-
-    chain(V.memset(T.msk[:, 0:512], 1.0))
+    chain(V.memset(T.msk[0:32, 0:512], 1.0))
+    chain(V.memset(T.val[0:32, 0:512], 0.0))
     chained()
-    chain(V.memset(T.msk[:, 0:512:32], 0.0))
+    chain(V.memset(T.msk[0:32, 0:512:32], 0.0))
     V.wait_ge(sem.iota, 2)
     chain(V.tensor_scalar(T.p15[:, 0:32], T.iop[:, 0:32], 15, None, AluOpType.bitwise_and))
-    chain(V.tensor_scalar(T.sidi[:, 0:1], T.iop[:, 0:1], 31, None, AluOpType.bitwise_and))
+    chain(V.tensor_copy(T.part[:, 0:1], T.iop[:, 0:1]))
     chained()
     chain(V.tensor_tensor(T.obase[:, 0:32], T.ioa[:, 0:32], T.p15[:, 0:32], add))
-    chain(V.tensor_copy(T.sidf[:, 0:1], T.sidi[:, 0:1]))
+    V.wait_ge(sem.pbo, 1)
+    V.tensor_scalar(T.tbl[:, 0:16], T.tall[:, 0:16], 0, 512, maxi, mult).then_inc(sem.tbr, 1)
+    chain(V.tensor_scalar(T.om[:, 0:2], T.tall[:, 2 * rank:2 * rank + 2], 0, 128, maxi, mult))
+    chained()
+    V.tensor_tensor(T.oidx[:, 0:2], T.om[:, 0:2], T.iop[:, 0:2], add).then_inc(sem.oid, 1)
+    V.wait_ge(sem.s_ad, 32)
+    chain(V.tensor_copy(T.ab[0:32, 0:32], T.adt[0:32, 0:32]))
+    chain(V.tensor_scalar(T.adm[0:32, 0:32], T.adt[0:32, 0:32], 128, -1, mult, add))
+    chained()
+    V.transpose(T.at[0:32, 0:32], T.ab[0:32, 0:32]).then_inc(sem.atd, 1)
     V.wait_ge(sem.s_tok, 128)
     V.tensor_scalar(T.offx[:, 0:128], T.tokt[:, 0:128], 0, 4, maxi, mult).then_inc(sem.offx, 1)
-    V.wait_ge(sem.offx, 1)
-    V.wait_ge(sem.s_x, 16)
-    first = True
-    for h in X_EARLY:
-        for t in X_VEC[h]:
-            gather_x("v", h, t)
-            if first:
-                first = False
-                V.wait_ge(sem.pbo, 1)
-                chain(V.tensor_scalar(T.om[:, 0:2], T.oall[:, 0:2], 0, 128, maxi, mult))
-                chained()
-                V.tensor_tensor(T.oidx[:, 0:2], T.om[:, 0:2], T.iop[:, 0:2], add).then_inc(sem.oid, 1)
-    V.wait_ge(sem.s_ad, 128)
-    chain(V.tensor_copy(T.ab[:, 0:32], T.adt[:, 0:32]))
-    chain(V.tensor_scalar(T.adm[:, 0:32], T.adt[:, 0:32], 128, -1, mult, add))
-    chained()
-    V.transpose(T.at[:, 0:32], T.ab[:, 0:32]).then_inc(sem.atd, 1)
 
-    def load_table(n, a, b):
-        V.wait_ge(sem["pb%d" % n], 1)
-        chain(V.tensor_scalar(T.mf[:, a:b], T.mall[:, a:b], 0, 512, maxi, mult))
+    def places():
+        V.wait_ge(sem.s_adb, 256)
+        chain(V.tensor_scalar(T.eq[0:16, 0:512], T.adb[0:16, 0:512], T.part[0:16, 0:1], None, AluOpType.is_equal))
         chained()
+        chain(V.tensor_tensor_scan(T.cnt[0:16, 0:512], T.eq[0:16, 0:512], T.eq[0:16, 0:512], 0.0, add, maxi))
+        chained()
+        for b in range(16):
+            chain(V.tensor_tensor(T.val[0:16, 32 * b:32 * b + 32], T.eq[0:16, b:512:16], T.cnt[0:16, b:512:16], mult))
+        chained()
+        chain(V.transpose(T.trb[0:32, 0:512], T.val[0:32, 0:512]))
+        chained()
+        chain(V.tensor_tensor_scan(T.sc[0:32, 0:512], T.msk[0:32, 0:512], T.trb[0:32, 0:512], 0.0, mult, add))
+        chained()
+        for c in range(2):
+            chain(V.tensor_copy(T.r2[0:32, 16 * c:16 * c + 16], T.sc[0:32, 31:512:32]))
+        chained()
+        chain(V.transpose(T.ot[0:32, 0:32], T.r2[0:32, 0:32]))
+        chained()
+        chain(V.tensor_tensor(T.posf[0:32, 0:32], T.adm[0:32, 0:32], T.ot[0:32, 0:32], add))
+        chained()
+        V.tensor_copy(T.posl[0:32, 0:32], T.posf[0:32, 0:32]).then_inc(sem.pos, 1)
 
-    def offsets_of(i, who):
-        for k in range(2):
-            j = 2 * i + k
-            if (k in S_TILES[i]) == (who == "s"):
-                V.tensor_scalar(T.off[:, 32 * j:32 * j + 32], T.obase[:, 0:32], T.mf[:, j:j + 1], None, add).then_inc(sem["of%d" % j], 1)
+    ready = set()
 
-    def gather_v(i):
-        for k in range(2):
-            if k not in S_TILES[i]:
+    def once(eng, key, name, n):
+        if (key, name) not in ready:
+            ready.add((key, name))
+            eng.wait_ge(sem[name], n)
+
+    def work(eng, key, words):
+        def move(out, in_):
+            return V.tensor_copy(out, in_) if key == "v" else S.activation(out, in_, copy)
+        for word in words.split():
+            w = word.split(".")
+            a = [int(c) for c in w[1:]]
+            if w[0] == "x":
+                h, t = a
+                b = (rank & ~1) ^ (2 * h)
+                once(eng, key, "offx", 1)
+                once(eng, key, "s_x", 16)
+                move(T.xgt[:, 2048 * h + t:2048 * h + 2048:4],
+                     T.xin[:, t:2048].indirect(T.offx[:, 16 * b:16 * b + 32])).then_inc(sem["xg%d" % h], 1)
+            elif w[0] == "z":
+                h, = a
+                V.wait_ge(sem["xg%d" % h], 4)
+                V.quantize_mx(T.xq[:, 512 * h:512 * h + 512], T.xp[:, 512 * h:512 * h + 512],
+                              T.xgt[:, 2048 * h:2048 * h + 2048]).then_inc(sem["xz%d" % h], 1)
+            elif w[0] == "o":
+                i, = a
+                V.wait_ge(sem["tb%d" % i], tables[i])
+                for j in (2 * i + 1, 2 * i):
+                    V.tensor_scalar(T.off[:, 32 * j:32 * j + 32], T.obase[:, 0:32], T.mrec[:, j:j + 1], None, add).then_inc(sem["of%d" % i], 1)
+            elif w[0] == "v":
+                i, k = a
                 j = 2 * i + k
-                V.wait_ge(sem["of%d" % j], 1)
-                V.tensor_copy(T.ag[:, 512 * j:512 * j + 512], tile_window(j)).then_inc(sem["vg%d" % i], 1)
+                once(eng, key, "s_wa", 128)
+                once(eng, key, "of%d" % i, 2)
+                move(T.agt[:, 512 * j:512 * j + 512],
+                     T.win[:, 0:4096].indirect(T.off[:, 32 * j:32 * j + 32])).then_inc(sem["tg%d" % i], 1)
+            elif w[0] == "q":
+                i, = a
+                V.wait_ge(sem["tg%d" % i], 2)
+                V.quantize_mx(T.cs[:, 256 * i:256 * i + 256], T.ps[:, 256 * i:256 * i + 256],
+                              T.agt[:, 1024 * i:1024 * i + 1024]).then_inc(sem["q%d" % i], 1)
+            elif w[0] == "w":
+                V.wait_ge(sem.s_own, 32)
+                V.quantize_mx(T.oc[:, 0:256], T.op[:, 0:256], T.own[:, 0:1024]).then_inc(sem.qo, 1)
+            elif w[0] == "r":
+                places()
+            else:
+                n, k = a
+                i = PRODUCTS[n]
+                s = 2 * (rank if i == 7 else rank ^ ORDER[i]) + k
+                bank = 2 * (n % 4) + k
+                eng.wait_ge(sem["m%d_%d" % (k, n)], 1)
+                move(T.res[:, 128 * s:128 * s + 128], T.acc[:, 512 * bank:512 * bank + 128]).then_inc(sem["e%d_%d" % (k, n)], 1)
 
-    def quant_tile(i):
-        if len(S_TILES[i]) < 2:
-            V.wait_ge(sem["vg%d" % i], 2 - len(S_TILES[i]))
-        V.wait_ge(sem["sg%d" % i], len(S_TILES[i]))
-        V.quantize_mx(T.cs[:, 256 * i:256 * i + 256], T.ps[:, 256 * i:256 * i + 256],
-                      T.ag[:, 1024 * i:1024 * i + 1024]).then_inc(sem["q%d" % i], 1)
+    work(V, "v", VECTOR)
+    work(S, "s", SCALAR)
 
-    load_table(1, 0, 2 * EARLY)
-    offsets_of(0, "s")
-    offsets_of(0, "v")
-    offsets_of(1, "s")
-    V.wait_ge(sem.s_wa, 128)
-    gather_v(0)
-    offsets_of(1, "v")
-    offsets_of(2, "s")
-    quant_tile(0)
-    gather_v(1)
-    load_table(2, 2 * EARLY, 14)
-    offsets_of(3, "s")
-    offsets_of(3, "v")
-    quant_tile(1)
-    gather_v(3)
-    offsets_of(4, "s")
-    offsets_of(4, "v")
-    offsets_of(5, "s")
-    quant_tile(2)
-    gather_v(4)
-    offsets_of(6, "s")
-    offsets_of(6, "v")
-    quant_tile(3)
-    quant_tile(4)
-    gather_v(6)
-    quant_tile(5)
-    quant_tile(6)
-
-    for h in X_EARLY:
-        quant_x(h)
-    V.wait_ge(sem.s_own, 32)
-    V.quantize_mx(T.oc[:, 0:256], T.op[:, 0:256], T.own[:, 0:1024]).then_inc(sem.qo, 1)
-    for h in X_LATE:
-        for t in X_VEC[h]:
-            gather_x("v", h, t)
-    evacuate("v", 0)
-    evacuate("v", 1)
-    V.wait_ge(sem.pba, 1)
-    chain(V.tensor_scalar(T.eq[:, 0:512], T.adb[:, 0:512], T.sidf[:, 0:1], None, AluOpType.is_equal))
-    chained()
-    chain(V.tensor_tensor_scan(T.cnt[:, 0:512], T.eq[:, 0:512], T.eq[:, 0:512], 0.0, add, maxi))
-    chained()
-    for b in range(16):
-        chain(V.tensor_tensor(T.val[:, 32 * b:32 * b + 32], T.eq[:, b:512:16], T.cnt[:, b:512:16], mult))
-    chained()
-    chain(V.transpose(T.trb[:, 0:512], T.val[:, 0:512]))
-    chained()
-    chain(V.tensor_tensor_scan(T.sc[:, 0:512], T.msk[:, 0:512], T.trb[:, 0:512], 0.0, mult, add))
-    chained()
-    for c in range(2):
-        chain(V.tensor_copy(T.r2[:, 16 * c:16 * c + 16], T.sc[:, 31:512:32]))
-    chained()
-    chain(V.transpose(T.ot[:, 0:32], T.r2[:, 0:32]))
-    chained()
-    chain(V.tensor_tensor(T.posf[:, 0:32], T.adm[:, 0:32], T.ot[:, 0:32], add))
-    chained()
-    V.tensor_copy(T.posu[:, 0:32], T.posf[:, 0:32]).then_inc(sem.pos, 1)
-    for h in X_LATE:
-        quant_x(h)
-    for n in range(2, 8):
-        evacuate("v", n)
-
-    S.wait_ge(sem.offx, 1)
-    S.wait_ge(sem.s_x, 16)
-    for h in X_EARLY:
-        for t in range(4):
-            if t not in X_VEC[h]:
-                gather_x("s", h, t)
-    S.wait_ge(sem.s_wa, 128)
-    for i in range(7):
-        for k in S_TILES[i]:
-            j = 2 * i + k
-            S.wait_ge(sem["of%d" % j], 1)
-            S.activation(T.ag[:, 512 * j:512 * j + 512], tile_window(j), copy).then_inc(sem["sg%d" % i], 1)
-    for h in X_LATE:
-        for t in range(4):
-            if t not in X_VEC[h]:
-                gather_x("s", h, t)
-    for n in range(8):
-        evacuate("s", n)
-
-    seen = set()
     for n, i in enumerate(PRODUCTS):
         d = 0 if i == 7 else ORDER[i]
-        if d >> 1 not in seen:
-            seen.add(d >> 1)
-            P.wait_ge(sem["xz%d" % (d >> 1)], 1)
+        once(P, "p", "xz%d" % (d >> 1), 1)
         if i == 7:
             P.wait_ge(sem.qo, 1)
         else:
@@ -339,18 +318,18 @@ def rank_program(g, core, T, topo):
         for k in range(2):
             bank = 2 * (n % 4) + k
             if n >= 4:
-                P.wait_ge(sem["%s%d" % (("ev", "es")[k], n - 4)], 1)
+                P.wait_ge(sem["e%d_%d" % (k, n - 4)], 1)
             a = 512 * (d >> 1) + 256 * ((rank ^ d) & 1) + 128 * k
             c = 128 * k if i == 7 else 256 * i + 128 * k
             w, ws = (T.oc, T.op) if i == 7 else (T.cr, T.pr)
             P.matmul_mx(T.acc[:, 512 * bank:512 * bank + 128], w[:, c:c + 128], ws[:, c:c + 128],
-                        T.xq[:, a:a + 128], T.xp[:, a:a + 128], True, True).then_inc(sem["%s%d" % (("mv", "ms")[k], n)], 1)
+                        T.xq[:, a:a + 128], T.xp[:, a:a + 128], True, True).then_inc(sem["m%d_%d" % (k, n)], 1)
 
     for eng in (V, S):
-        eng.wait_ge(sem.pos, 1)
+        eng.wait_ge(sem.s_pos, 64)
         for n in range(8):
-            eng.wait_ge(sem["ev%d" % n], 1)
-            eng.wait_ge(sem["es%d" % n], 1)
+            eng.wait_ge(sem["e0_%d" % n], 1)
+            eng.wait_ge(sem["e1_%d" % n], 1)
     V.tensor_copy(T.ysb[:, 0:256], T.res[:, 0:2048].indirect(T.posu[:, 0:16])).then_inc(sem.fv, 1)
     S.activation(T.ysb[:, 256:512], T.res[:, 0:2048].indirect(T.posu[:, 16:32]), copy).then_inc(sem.fs, 1)
     Y.wait_ge(sem.fv, 1)

from concourse.bass import DstId, RemoteDMATransfer, IndirectOffsetOnAxis
from concourse.mybir import dt, AluOpType, ActivationFunctionType

ORDER = (4, 2, 5, 3, 6, 7, 1)
RELAY = ()
TABLES = ((0, 1), (2, 3), (4, 5, 6))
SENDS = ((0,), (1, 2), (3, 4), (5,), (6,))
PRODUCTS = (0, 1, 2, 3, 4, 6, 7, 5)
VECTOR = ("x.2.0 x.2.1 x.1.0 x.1.1 o.0 o.1 v.0.0 o.2 q.0 v.1.0 o.3 q.1 v.3.0 o.4 q.2 o.5 v.4.0 q.3 o.6 q.4 v.6.0 q.5 q.6 "
          "z.2 z.1 w x.3.0 e.0.0 r z.3 z.0 e.1.0 e.2.0 e.3.0 e.4.0 e.5.0 e.6.0 e.7.0")
SCALAR = ("x.2.2 x.2.3 x.1.2 x.1.3 v.0.1 v.1.1 v.2.0 v.2.1 v.3.1 v.4.1 v.5.0 v.5.1 v.6.1 x.3.1 x.3.2 x.3.3 x.0.0 x.0.1 x.0.2 x.0.3 "
          "e.0.1 e.1.1 e.2.1 e.3.1 e.4.1 e.5.1 e.6.1 e.7.1")
GPSIMD = "i.0 i.1 s.0 s.1 s.2 s.3 s.4"
LOADS_SYNC = "o a.0 t.0 t.2 t.4 t.6 w.0 w.2 w.4 w.6"
LOADS_SCALAR = "a.1 t.1 t.3 t.5 t.7 x w.1 w.3 w.5 w.7"

SCRATCH = {
    "orow": ("sbuf", [128, 16], "int32"),
    "tall": ("sbuf", [128, 16], "int32"),
    "tbl": ("sbuf", [128, 16], "bfloat16"),
    "mrec": ("sbuf", [128, 16], "bfloat16"),
    "om": ("sbuf", [128, 2], "int32"),
    "oidx": ("sbuf", [128, 2], "int32"),
    "own": ("sbuf", [128, 1024], "bfloat16"),
    "ioa": ("sbuf", [128, 32], "int32"),
    "iop": ("sbuf", [128, 32], "int32"),
    "part": ("sbuf", [128, 2], "float32"),
    "p15": ("sbuf", [128, 32], "int32"),
    "obase": ("sbuf", [128, 32], "int32"),
    "off": ("sbuf", [128, 32 * 14], "uint16"),
    "win": ("sbuf", [128, 4096], "bfloat16"),
    "agt": ("sbuf", [128, 1024 * 7], "bfloat16"),
    "cs": ("sbuf", [128, 256 * 7], "float8_e4m3fn_x4"),
    "ps": ("sbuf", [128, 256 * 7], "uint8"),
    "cr": ("sbuf", [128, 256 * 7], "float8_e4m3fn_x4"),
    "pr": ("sbuf", [128, 256 * 7], "uint8"),
    "hc": ("sbuf", [128, 256], "float8_e4m3fn_x4"),
    "hp": ("sbuf", [128, 256], "uint8"),
    "oc": ("sbuf", [128, 256], "float8_e4m3fn_x4"),
    "op": ("sbuf", [128, 256], "uint8"),
    "xin": ("sbuf", [128, 2048], "bfloat16"),
    "tokt": ("sbuf", [128, 128], "int32"),
    "offx": ("sbuf", [128, 128], "uint16"),
    "xgt": ("sbuf", [128, 8192], "bfloat16"),
    "xq": ("sbuf", [128, 2048], "float8_e4m3fn_x4"),
    "xp": ("sbuf", [128, 2048], "uint8"),
    "adt": ("sbuf", [128, 32], "int32"),
    "ab": ("sbuf", [128, 32], "bfloat16"),
    "at": ("sbuf", [128, 32], "bfloat16"),
    "adb": ("sbuf", [128, 512], "bfloat16"),
    "eq": ("sbuf", [128, 512], "bfloat16"),
    "cnt": ("sbuf", [128, 512], "bfloat16"),
    "val": ("sbuf", [128, 512], "bfloat16"),
    "trb": ("sbuf", [128, 512], "bfloat16"),
    "msk": ("sbuf", [128, 512], "bfloat16"),
    "sc": ("sbuf", [128, 512], "bfloat16"),
    "r2": ("sbuf", [128, 32], "bfloat16"),
    "ot": ("sbuf", [128, 32], "bfloat16"),
    "adm": ("sbuf", [128, 32], "float32"),
    "posf": ("sbuf", [128, 32], "float32"),
    "posl": ("sbuf", [128, 32], "uint16"),
    "posu": ("sbuf", [128, 32], "uint16"),
    "acc": ("psum", [128, 4096], "float32"),
    "res": ("sbuf", [128, 2048], "float32"),
    "ysb": ("sbuf", [128, 512], "float32"),
}
SEMAPHORES = (["s_orow", "s_tok", "s_x", "s_wa", "s_ad", "s_adb", "s_own", "s_pos", "s_y1", "s_y2", "hrc", "hrp",
               "iota", "pbo", "vc", "tbr", "offx", "oid", "atd", "qo", "pos", "fv", "fs", "sent"]
              + ["%s%d" % (n, i) for n in ("tb", "of", "tg", "q", "arr") for i in range(7)]
              + ["%s%d" % (n, i) for n in ("xg", "xz") for i in range(4)]
              + ["%s%d" % (n, i) for n in ("m0_", "m1_", "e0_", "e1_") for i in range(8)])


def bits(engines):
    return sum(1 << e for e in engines)


def address(topo, to, core):
    rid, pid = topo.addr(to, core)
    return DstId(rid=rid, pnc=pid)


def engine_sets(T, topo, core):
    near = topo.cores_of(core)
    wide = sorted({e for c in T.cores if c not in near for e in topo.engines(core, c)})
    inner = sorted({e for c in near if c != core for e in topo.engines(core, c)} - set(wide))
    return wide, inner[:len(inner) // 2]


def helpers(T, topo, rank):
    core, taken = T.cores[rank], {}
    for i in RELAY:
        to = T.cores[rank ^ ORDER[i]]
        free = [h for h in topo.cores_of(core) if h not in T.cores and h not in taken.values()
                and topo.die(h) == topo.die(core) and topo.may_write(core, h) and topo.may_write(h, to)]
        taken[i] = min(free, key=lambda h: (sum(topo.may_write(h, c) for c in T.cores), h))
    return taken


def relay_program(g, core, T, topo):
    for rank in range(len(T.cores)):
        for i, h in helpers(T, topo, rank).items():
            if h == core:
                to = T.cores[rank ^ ORDER[i]]
                out, here = topo.engines(core, to), len(engine_sets(T, topo, T.cores[rank])[1])
                for name, a, b in (("hrc", T.hc[:, 0:256].bitcast(dt.uint8), T.cr[:, 256 * i:256 * i + 256].bitcast(dt.uint8)),
                                   ("hrp", T.hp[:, 0:256], T.pr[:, 256 * i:256 * i + 256])):
                    g.wait_ge(T.sem[name], here)
                    g.remote_dma_fused([RemoteDMATransfer(dst_ids=[address(topo, to, core)], dma_engine_mask=bits(out),
                                                          remote_sem=T.sem["arr%d" % i], srcs=[a], dsts=[b])], local_sem=T.sem.sent)
                g.wait_ge(T.sem.sent, 2 * len(out))


def rank_program(g, core, T, topo):
    rank = T.rank_of(core)
    if rank is None:
        relay_program(g, core, T, topo)
        return
    V, S, P, Y, sem = g.vector, g.scalar, g.tensor, g.sync, T.sem
    add, mult, maxi = AluOpType.add, AluOpType.mult, AluOpType.max
    copy = ActivationFunctionType.Copy
    peers = [T.cores[rank ^ d] for d in ORDER]
    helper = helpers(T, topo, rank)
    wide, inner = engine_sets(T, topo, core)

    def share(group, relays=()):
        out = [i for i in group if peers[i] not in topo.cores_of(core) and i not in relays]
        per = len(wide) // max(1, len(out))
        m = {i: wide[per * n:per * n + per] for n, i in enumerate(out)}
        m.update({i: inner for i in group if i not in out})
        return m

    vn = [0]

    def chain(ins):
        ins.then_inc(sem.vc, 1)
        vn[0] += 1

    def chained():
        V.wait_ge(sem.vc, vn[0])

    for eng, words in ((Y, LOADS_SYNC), (S, LOADS_SCALAR)):
        for word in words.split():
            w = word.split(".")
            c = int(w[1]) if len(w) > 1 else 0
            if w[0] == "o":
                eng.dma_start(T.orow[0:1, 0:16], T.tab[:, :]).then_inc(sem.s_orow, 16)
            elif w[0] == "t":
                eng.dma_start(T.tokt[16 * c:16 * c + 16, :], T.tok[:, :]).then_inc(sem.s_tok, 16)
            elif w[0] == "a":
                eng.dma_start(T.adt[16 * c:16 * c + 16, :], T.ad[:, :]).then_inc(sem.s_ad, 16)
            elif w[0] == "x":
                eng.dma_start(T.xin[:, :], T.x[:, :]).then_inc(sem.s_x, 16)
            else:
                eng.dma_start(T.win[:, 512 * c:512 * c + 512], T.wa[128 * c:128 * c + 128, :]).then_inc(sem.s_wa, 16)
    Y.wait_ge(sem.atd, 1)
    for s in range(16):
        Y.dma_start(T.adb[s:s + 1, 0:512], T.at[0:32, 0:16]).then_inc(sem.s_adb, 16)
    Y.wait_ge(sem.pos, 1)
    for c in range(4):
        Y.dma_start(T.posu[32 * c:32 * c + 32, :], T.posl[0:32, :]).then_inc(sem.s_pos, 16)

    g.iota(T.ioa[:, 0:32], [[16, 32]], 0, 0).then_inc(sem.iota, 1)
    g.iota(T.iop[:, 0:32], [[0, 32]], 0, 1).then_inc(sem.iota, 1)
    g.wait_ge(sem.s_orow, 16)
    g.partition_broadcast(T.tall[:, 0:16], T.orow[0:1, 0:16], 128).then_inc(sem.pbo, 1)
    g.wait_ge(sem.tbr, 1)
    nsent = 0
    tables, arrived = {}, {}
    for group in TABLES:
        moves = []
        for i, engs in share(group).items():
            p = rank ^ ORDER[i]
            moves.append(RemoteDMATransfer(dst_ids=[address(topo, peers[i], core)], dma_engine_mask=bits(engs),
                                           remote_sem=sem["tb%d" % i], srcs=[T.tbl[:, 2 * p:2 * p + 2]],
                                           dsts=[T.mrec[:, 2 * i:2 * i + 2]]))
            tables[i] = len(engs)
            nsent += len(engs)
        g.remote_dma_fused(moves, local_sem=sem.sent)
    for word in GPSIMD.split():
        w = word.split(".")
        if w[0] == "i":
            k = int(w[1])
            g.wait_ge(sem.oid, 1)
            g.indirect_dma_start(T.own[:, 512 * k:512 * k + 512], None, T.wa[:],
                                 IndirectOffsetOnAxis(ap=T.oidx[:, k:k + 1], axis=0), bounds_check=1023).then_inc(sem.s_own, 16)
            continue
        group = SENDS[int(w[1])]
        for i in group:
            g.wait_ge(sem["q%d" % i], 1)
        for codes in (True, False):
            moves = []
            for i, engs in share(group, RELAY).items():
                a = (T.cs if codes else T.ps)[:, 256 * i:256 * i + 256]
                if i in RELAY:
                    b, to, name = (T.hc if codes else T.hp)[:, 0:256], helper[i], "hrc" if codes else "hrp"
                    arrived[i] = 2 * len(topo.engines(helper[i], peers[i]))
                else:
                    b, to, name = (T.cr if codes else T.pr)[:, 256 * i:256 * i + 256], peers[i], "arr%d" % i
                    arrived[i] = 2 * len(engs)
                if codes:
                    a, b = a.bitcast(dt.uint8), b.bitcast(dt.uint8)
                moves.append(RemoteDMATransfer(dst_ids=[address(topo, to, core)], dma_engine_mask=bits(engs),
                                               remote_sem=sem[name], srcs=[a], dsts=[b]))
                nsent += len(engs)
            g.remote_dma_fused(moves, local_sem=sem.sent)
    g.wait_ge(sem.sent, nsent)

    chain(V.memset(T.msk[0:32, 0:512], 1.0))
    chain(V.memset(T.val[0:32, 0:512], 0.0))
    chained()
    chain(V.memset(T.msk[0:32, 0:512:32], 0.0))
    V.wait_ge(sem.iota, 2)
    chain(V.tensor_scalar(T.p15[:, 0:32], T.iop[:, 0:32], 15, None, AluOpType.bitwise_and))
    chain(V.tensor_copy(T.part[:, 0:1], T.iop[:, 0:1]))
    chained()
    chain(V.tensor_tensor(T.obase[:, 0:32], T.ioa[:, 0:32], T.p15[:, 0:32], add))
    V.wait_ge(sem.pbo, 1)
    V.tensor_scalar(T.tbl[:, 0:16], T.tall[:, 0:16], 0, 512, maxi, mult).then_inc(sem.tbr, 1)
    chain(V.tensor_scalar(T.om[:, 0:2], T.tall[:, 2 * rank:2 * rank + 2], 0, 128, maxi, mult))
    chained()
    V.tensor_tensor(T.oidx[:, 0:2], T.om[:, 0:2], T.iop[:, 0:2], add).then_inc(sem.oid, 1)
    V.wait_ge(sem.s_ad, 32)
    chain(V.tensor_copy(T.ab[0:32, 0:32], T.adt[0:32, 0:32]))
    chain(V.tensor_scalar(T.adm[0:32, 0:32], T.adt[0:32, 0:32], 128, -1, mult, add))
    chained()
    V.transpose(T.at[0:32, 0:32], T.ab[0:32, 0:32]).then_inc(sem.atd, 1)
    V.wait_ge(sem.s_tok, 128)
    V.tensor_scalar(T.offx[:, 0:128], T.tokt[:, 0:128], 0, 4, maxi, mult).then_inc(sem.offx, 1)

    def places():
        V.wait_ge(sem.s_adb, 256)
        chain(V.tensor_scalar(T.eq[0:16, 0:512], T.adb[0:16, 0:512], T.part[0:16, 0:1], None, AluOpType.is_equal))
        chained()
        chain(V.tensor_tensor_scan(T.cnt[0:16, 0:512], T.eq[0:16, 0:512], T.eq[0:16, 0:512], 0.0, add, maxi))
        chained()
        for b in range(16):
            chain(V.tensor_tensor(T.val[0:16, 32 * b:32 * b + 32], T.eq[0:16, b:512:16], T.cnt[0:16, b:512:16], mult))
        chained()
        chain(V.transpose(T.trb[0:32, 0:512], T.val[0:32, 0:512]))
        chained()
        chain(V.tensor_tensor_scan(T.sc[0:32, 0:512], T.msk[0:32, 0:512], T.trb[0:32, 0:512], 0.0, mult, add))
        chained()
        for c in range(2):
            chain(V.tensor_copy(T.r2[0:32, 16 * c:16 * c + 16], T.sc[0:32, 31:512:32]))
        chained()
        chain(V.transpose(T.ot[0:32, 0:32], T.r2[0:32, 0:32]))
        chained()
        chain(V.tensor_tensor(T.posf[0:32, 0:32], T.adm[0:32, 0:32], T.ot[0:32, 0:32], add))
        chained()
        V.tensor_copy(T.posl[0:32, 0:32], T.posf[0:32, 0:32]).then_inc(sem.pos, 1)

    ready = set()

    def once(eng, key, name, n):
        if (key, name) not in ready:
            ready.add((key, name))
            eng.wait_ge(sem[name], n)

    def work(eng, key, words):
        def move(out, in_):
            return V.tensor_copy(out, in_) if key == "v" else S.activation(out, in_, copy)
        for word in words.split():
            w = word.split(".")
            a = [int(c) for c in w[1:]]
            if w[0] == "x":
                h, t = a
                b = (rank & ~1) ^ (2 * h)
                once(eng, key, "offx", 1)
                once(eng, key, "s_x", 16)
                move(T.xgt[:, 2048 * h + t:2048 * h + 2048:4],
                     T.xin[:, t:2048].indirect(T.offx[:, 16 * b:16 * b + 32])).then_inc(sem["xg%d" % h], 1)
            elif w[0] == "z":
                h, = a
                V.wait_ge(sem["xg%d" % h], 4)
                V.quantize_mx(T.xq[:, 512 * h:512 * h + 512], T.xp[:, 512 * h:512 * h + 512],
                              T.xgt[:, 2048 * h:2048 * h + 2048]).then_inc(sem["xz%d" % h], 1)
            elif w[0] == "o":
                i, = a
                V.wait_ge(sem["tb%d" % i], tables[i])
                for j in (2 * i + 1, 2 * i):
                    V.tensor_scalar(T.off[:, 32 * j:32 * j + 32], T.obase[:, 0:32], T.mrec[:, j:j + 1], None, add).then_inc(sem["of%d" % i], 1)
            elif w[0] == "v":
                i, k = a
                j = 2 * i + k
                once(eng, key, "s_wa", 128)
                once(eng, key, "of%d" % i, 2)
                move(T.agt[:, 512 * j:512 * j + 512],
                     T.win[:, 0:4096].indirect(T.off[:, 32 * j:32 * j + 32])).then_inc(sem["tg%d" % i], 1)
            elif w[0] == "q":
                i, = a
                V.wait_ge(sem["tg%d" % i], 2)
                V.quantize_mx(T.cs[:, 256 * i:256 * i + 256], T.ps[:, 256 * i:256 * i + 256],
                              T.agt[:, 1024 * i:1024 * i + 1024]).then_inc(sem["q%d" % i], 1)
            elif w[0] == "w":
                V.wait_ge(sem.s_own, 32)
                V.quantize_mx(T.oc[:, 0:256], T.op[:, 0:256], T.own[:, 0:1024]).then_inc(sem.qo, 1)
            elif w[0] == "r":
                places()
            else:
                n, k = a
                i = PRODUCTS[n]
                s = 2 * (rank if i == 7 else rank ^ ORDER[i]) + k
                bank = 2 * (n % 4) + k
                eng.wait_ge(sem["m%d_%d" % (k, n)], 1)
                move(T.res[:, 128 * s:128 * s + 128], T.acc[:, 512 * bank:512 * bank + 128]).then_inc(sem["e%d_%d" % (k, n)], 1)

    work(V, "v", VECTOR)
    work(S, "s", SCALAR)

    for n, i in enumerate(PRODUCTS):
        d = 0 if i == 7 else ORDER[i]
        once(P, "p", "xz%d" % (d >> 1), 1)
        if i == 7:
            P.wait_ge(sem.qo, 1)
        else:
            P.wait_ge(sem["arr%d" % i], arrived[i])
        for k in range(2):
            bank = 2 * (n % 4) + k
            if n >= 4:
                P.wait_ge(sem["e%d_%d" % (k, n - 4)], 1)
            a = 512 * (d >> 1) + 256 * ((rank ^ d) & 1) + 128 * k
            c = 128 * k if i == 7 else 256 * i + 128 * k
            w, ws = (T.oc, T.op) if i == 7 else (T.cr, T.pr)
            P.matmul_mx(T.acc[:, 512 * bank:512 * bank + 128], w[:, c:c + 128], ws[:, c:c + 128],
                        T.xq[:, a:a + 128], T.xp[:, a:a + 128], True, True).then_inc(sem["m%d_%d" % (k, n)], 1)

    for eng in (V, S):
        eng.wait_ge(sem.s_pos, 64)
        for n in range(8):
            eng.wait_ge(sem["e0_%d" % n], 1)
            eng.wait_ge(sem["e1_%d" % n], 1)
    V.tensor_copy(T.ysb[:, 0:256], T.res[:, 0:2048].indirect(T.posu[:, 0:16])).then_inc(sem.fv, 1)
    S.activation(T.ysb[:, 256:512], T.res[:, 0:2048].indirect(T.posu[:, 16:32]), copy).then_inc(sem.fs, 1)
    Y.wait_ge(sem.fv, 1)
    Y.dma_start(T.y[:, 0:256], T.ysb[:, 0:256]).then_inc(sem.s_y1, 16)
    S.wait_ge(sem.fs, 1)
    S.dma_start(T.y[:, 256:512], T.ysb[:, 256:512]).then_inc(sem.s_y2, 16)
    Y.wait_ge(sem.s_y1, 16)
    S.wait_ge(sem.s_y2, 16)
    V.wait_ge(sem.vc, vn[0])
